import numpy as np
import ml_dtypes


def mxq(x, axis, fmt="e4m3"):
    dtype, down = {"e4m3": (ml_dtypes.float8_e4m3fn, 7), "e5m2": (ml_dtypes.float8_e5m2, 14)}[fmt]
    v = np.moveaxis(np.asarray(x, np.float32).astype(ml_dtypes.bfloat16).astype(np.float64), axis, -1)
    blocks = v.reshape(v.shape[:-1] + (-1, 32))
    amax = np.abs(blocks).max(-1, keepdims=True)
    byte = np.maximum(np.where(amax > 0, np.frexp(amax)[1] - 1 + 127, 0) - down, 1)
    scale = np.exp2(byte - 127.0)
    codes = (blocks / scale).astype(np.float32).astype(dtype).astype(np.float64)
    return np.moveaxis((codes * scale).reshape(v.shape), -1, axis)


WIDE = False


def mx_kscale(k):
    if not WIDE:
        return np.ones(k)
    levels = np.array([10, -10, 5, -5, 0])
    if k % 512:
        return np.exp2(np.random.permutation(np.resize(levels, k // 32))).repeat(32)
    a = np.empty((k // 512, 16))
    for p in range(k // 512):
        a[p, :8] = np.random.permutation(np.resize(levels, 8))
        for g in range(8):
            far = levels[np.abs(levels - a[p, g]) >= 10]
            a[p, g + 8] = far[np.random.randint(len(far))]
    return np.exp2(a.ravel()).repeat(32)


def f64(x):
    return np.asarray(x).astype(np.float64)


def striped(idx):
    return np.tile(idx.reshape(-1, 16).T, (8, 1)).astype(np.uint16)


def unstriped(offs):
    return offs[:16].T.reshape(-1).astype(np.int64)


def relu2(v):
    return np.maximum(v, 0.0) ** 2


K, T, D, S, V, N = 512, 2048, 3, 1024, 512, 128


def setup_inputs():
    n = np.random.standard_normal
    s = mx_kscale(K)[:, None]
    return {
        "xT": (n((K, T)) * s).astype(np.float32),
        "w": (n((K, N)) / np.sqrt(K) / s).astype(np.float32),
        "b": (0.3 * n((N, 1))).astype(np.float32),
        "gate": np.tile(np.random.uniform(0.2, 1.0, (D, 1, V)) / np.sqrt(D), (1, N, 1)).astype(np.float32),
        "offs": striped(np.random.permutation(T)[:S]),
        "pos1": striped(np.random.permutation(S)[:V]),
        "pos2": striped(np.random.permutation(S)[:V]),
        "pos3": striped(np.random.permutation(S)[:V]),
    }


def reference(xT, w, b, gate, offs, pos1, pos2, pos3):
    idx = unstriped(offs)
    xq = mxq(f64(xT)[:, idx], 0, "e4m3")
    y = mxq(f64(w), 0, "e4m3").T @ xq
    y = relu2(y + f64(b))
    return sum(f64(gate[d]) * y[:, unstriped(p)] for d, p in enumerate((pos1, pos2, pos3)))

@@ -1,0 +1,142 @@
+from contextlib import ExitStack
+
+import concourse.mybir as mybir
+
+K, T, D, S, V, N = 512, 2048, 3, 1024, 512, 128
+P = 128
+FLOPS = 2 * K * N * S
+
+F32 = mybir.dt.float32
+BF16 = mybir.dt.bfloat16
+U32 = mybir.dt.uint32
+U16 = mybir.dt.uint16
+U8 = mybir.dt.uint8
+FP8X4 = mybir.dt.float8_e4m3fn_x4
+ACT = mybir.ActivationFunctionType
+ALU = mybir.AluOpType
+
+CHUNK = 512
+PIECES = ((0, 512), (512, 256), (768, 256))
+
+
+def tile_picked_sub_lin_relu2_sub_e_kernel(tc, xT, w, b, gate, offs, pos1, pos2, pos3, out):
+    nc = tc.nc
+    with ExitStack() as ctx:
+        keep = ctx.enter_context(tc.tile_pool(name="keep", bufs=1))
+        psum = ctx.enter_context(tc.psum_pool(name="psum", bufs=1))
+
+        raw = [[keep.tile([P, 2, CHUNK], F32, name=f"raw_{u}_{c}") for c in range(T // CHUNK)] for u in range(2)]
+        pairs = [keep.tile([P, T, 2], BF16, name=f"pairs_{u}", align_bytes=64) for u in range(2)]
+        offsets = keep.tile([P, S // 16], U16, name="offsets")
+        lists = [keep.tile([P, V // 16], U16, name=f"list_{d}") for d in range(D)]
+        gates = [keep.tile([P, V], F32, name=f"gate_{d}") for d in range(D)]
+        w_raw = keep.tile([P, 4, N], F32, name="w_raw")
+        w_grouped = keep.tile([P, N, 4], BF16, name="w_grouped", align_bytes=64)
+        w_codes = keep.tile([P, N], U32, name="w_codes", align_bytes=64)
+        w_scales = keep.tile([P, N], U8, name="w_scales", align_bytes=64)
+        bias = keep.tile([P, 1], F32, name="bias")
+        grouped = [keep.tile([P, n, 4], BF16, name=f"grouped_{i}", align_bytes=64) for i, (a, n) in enumerate(PIECES)]
+        codes = [keep.tile([P, n], U32, name=f"codes_{i}", align_bytes=64) for i, (a, n) in enumerate(PIECES)]
+        scales = [keep.tile([P, n], U8, name=f"scales_{i}", align_bytes=64) for i, (a, n) in enumerate(PIECES)]
+        rect = [keep.tile([P, n], F32, name=f"rect_{i}") for i, (a, n) in enumerate(PIECES)]
+        y = keep.tile([P, S], F32, name="y")
+        turns = [keep.tile([P, V], F32, name=f"turn_{d}") for d in range(D)]
+        partial = keep.tile([P, V], F32, name="partial")
+        result = keep.tile([P, V], F32, name="result")
+        acc = [psum.tile([P, n], F32, name=f"acc_{i}") for i, (a, n) in enumerate(PIECES)]
+
+        x_view = xT.rearrange("(p u j) t -> u p j t", u=2, j=2)
+        for u in range(2):
+            for c in range(T // CHUNK):
+                nc.sync.dma_start(raw[u][c][:], x_view[u, :, :, c * CHUNK : (c + 1) * CHUNK])
+            if u == 0:
+                nc.sync.dma_start(offsets[:], offs)
+        nc.sync.dma_start(w_raw[:], w.rearrange("(p j) n -> p j n", j=4))
+        nc.sync.dma_start(bias[:], b)
+        for d, pos in enumerate((pos1, pos2, pos3)):
+            nc.sync.dma_start(lists[d][:], pos)
+        for d in range(D):
+            nc.sync.dma_start(gates[d][:], gate[d])
+
+        def cast(engine, u, c, lo=0, hi=CHUNK):
+            dst = pairs[u][:, c * CHUNK + lo : c * CHUNK + hi, :]
+            src = raw[u][c][:, :, lo:hi].rearrange("p j t -> p t j")
+            if engine == "S":
+                nc.scalar.activation(dst, src, ACT.Copy)
+            else:
+                nc.vector.tensor_copy(dst, src)
+
+        def gather(u, i):
+            a, n = PIECES[i]
+            words = grouped[i][:].rearrange("p n k -> p (n k)").bitcast(U32).rearrange("p (n u) -> p n u", u=2)
+            window = pairs[u][:].rearrange("p t e -> p (t e)").bitcast(U32)
+            nc.vector.tensor_copy(words[:, :, u], window.indirect(offsets[:, a // 16 : (a + n) // 16]))
+
+        def quantize(i):
+            nc.vector.quantize_mx(
+                out=codes[i][:].bitcast(FP8X4), scales=scales[i][:], in_=grouped[i][:].rearrange("p n k -> p (n k)")
+            )
+
+        def multiply(i):
+            nc.tensor.matmul_mx(
+                out=acc[i][:],
+                lhsT=w_codes[:].bitcast(FP8X4),
+                lhsT_scale=w_scales[:],
+                rhs=codes[i][:].bitcast(FP8X4),
+                rhs_scale=scales[i][:],
+                start=True,
+                stop=True,
+            )
+
+        def relu(engine, i, lo, hi):
+            if engine == "S":
+                nc.scalar.activation(rect[i][:, lo:hi], acc[i][:, lo:hi], ACT.Relu, bias=bias[:, 0:1])
+            else:
+                nc.vector.tensor_scalar(rect[i][:, lo:hi], acc[i][:, lo:hi], bias[:, 0:1], 0.0, ALU.add, ALU.max)
+
+        def square(engine, i, lo, hi):
+            a, n = PIECES[i]
+            if engine == "S":
+                nc.scalar.activation(y[:, a + lo : a + hi], rect[i][:, lo:hi], ACT.Square)
+            else:
+                nc.vector.tensor_tensor(y[:, a + lo : a + hi], rect[i][:, lo:hi], rect[i][:, lo:hi], ALU.mult)
+
+        cast("S", 0, 0)
+        cast("V", 0, 1)
+        cast("S", 0, 2)
+        cast("V", 0, 3)
+        for i in range(3):
+            gather(0, i)
+        cast("S", 1, 0)
+        cast("S", 1, 1)
+        cast("V", 1, 2)
+        cast("V", 1, 3, 0, 352)
+        cast("S", 1, 3, 352, 512)
+        nc.scalar.activation(w_grouped[:], w_raw[:].rearrange("p j n -> p n j"), ACT.Copy)
+        gather(1, 0)
+        gather(1, 1)
+        nc.vector.quantize_mx(
+            out=w_codes[:].bitcast(FP8X4), scales=w_scales[:], in_=w_grouped[:].rearrange("p n j -> p (n j)")
+        )
+        quantize(0)
+        multiply(0)
+        relu("S", 0, 0, 512)
+        square("S", 0, 0, 512)
+        gather(1, 2)
+        quantize(1)
+        multiply(1)
+        quantize(2)
+        multiply(2)
+        relu("V", 1, 0, 256)
+        relu("V", 2, 0, 256)
+        square("V", 1, 0, 256)
+        square("V", 2, 0, 256)
+
+        for d in range(D):
+            nc.vector.tensor_tensor(turns[d][:], y[:].indirect(lists[d][:]), gates[d][:], ALU.mult)
+        halves = (slice(0, 256), slice(256, 512))
+        for h in halves:
+            nc.vector.tensor_tensor(partial[:, h], turns[0][:, h], turns[1][:, h], ALU.add)
+        for h in halves:
+            nc.vector.tensor_tensor(result[:, h], partial[:, h], turns[2][:, h], ALU.add)
+            nc.sync.dma_start(out[:, h], result[:, h])

@@ -15,7 +15,7 @@ FP8X4 = mybir.dt.float8_e4m3fn_x4
 ACT = mybir.ActivationFunctionType
 ALU = mybir.AluOpType
 
-CHUNK = 512
+LOADS = (((0, 1024), (1024, 1024)), ((0, 1024), (1024, 512), (1536, 512)))
 PIECES = ((0, 512), (512, 256), (768, 256))
 
 
@@ -25,7 +25,7 @@ def tile_picked_sub_lin_relu2_sub_e_kernel(tc, xT, w, b, gate, offs, pos1, pos2,
         keep = ctx.enter_context(tc.tile_pool(name="keep", bufs=1))
         psum = ctx.enter_context(tc.psum_pool(name="psum", bufs=1))
 
-        raw = [[keep.tile([P, 2, CHUNK], F32, name=f"raw_{u}_{c}") for c in range(T // CHUNK)] for u in range(2)]
+        raw = [[keep.tile([P, 2, n], F32, name=f"raw_{u}_{a}") for (a, n) in LOADS[u]] for u in range(2)]
         pairs = [keep.tile([P, T, 2], BF16, name=f"pairs_{u}", align_bytes=64) for u in range(2)]
         offsets = keep.tile([P, S // 16], U16, name="offsets")
         lists = [keep.tile([P, V // 16], U16, name=f"list_{d}") for d in range(D)]
@@ -47,8 +47,8 @@ def tile_picked_sub_lin_relu2_sub_e_kernel(tc, xT, w, b, gate, offs, pos1, pos2,
 
         x_view = xT.rearrange("(p u j) t -> u p j t", u=2, j=2)
         for u in range(2):
-            for c in range(T // CHUNK):
-                nc.sync.dma_start(raw[u][c][:], x_view[u, :, :, c * CHUNK : (c + 1) * CHUNK])
+            for c, (a, n) in enumerate(LOADS[u]):
+                nc.sync.dma_start(raw[u][c][:], x_view[u, :, :, a : a + n])
             if u == 0:
                 nc.sync.dma_start(offsets[:], offs)
         nc.sync.dma_start(w_raw[:], w.rearrange("(p j) n -> p j n", j=4))
@@ -58,8 +58,9 @@ def tile_picked_sub_lin_relu2_sub_e_kernel(tc, xT, w, b, gate, offs, pos1, pos2,
         for d in range(D):
             nc.sync.dma_start(gates[d][:], gate[d])
 
-        def cast(engine, u, c, lo=0, hi=CHUNK):
-            dst = pairs[u][:, c * CHUNK + lo : c * CHUNK + hi, :]
+        def cast(engine, u, c, lo, hi):
+            a, n = LOADS[u][c]
+            dst = pairs[u][:, a + lo : a + hi, :]
             src = raw[u][c][:, :, lo:hi].rearrange("p j t -> p t j")
             if engine == "S":
                 nc.scalar.activation(dst, src, ACT.Copy)
@@ -101,17 +102,17 @@ def tile_picked_sub_lin_relu2_sub_e_kernel(tc, xT, w, b, gate, offs, pos1, pos2,
             else:
                 nc.vector.tensor_tensor(y[:, a + lo : a + hi], rect[i][:, lo:hi], rect[i][:, lo:hi], ALU.mult)
 
-        cast("S", 0, 0)
-        cast("V", 0, 1)
-        cast("S", 0, 2)
-        cast("V", 0, 3)
+        cast("S", 0, 0, 0, 640)
+        cast("V", 0, 0, 640, 1024)
+        cast("S", 0, 1, 0, 352)
+        cast("V", 0, 1, 352, 1024)
         for i in range(3):
             gather(0, i)
-        cast("S", 1, 0)
-        cast("S", 1, 1)
-        cast("V", 1, 2)
-        cast("V", 1, 3, 0, 352)
-        cast("S", 1, 3, 352, 512)
+        cast("S", 1, 0, 0, 512)
+        cast("S", 1, 0, 512, 1024)
+        cast("V", 1, 1, 0, 512)
+        cast("V", 1, 2, 0, 352)
+        cast("S", 1, 2, 352, 512)
         nc.scalar.activation(w_grouped[:], w_raw[:].rearrange("p j n -> p n j"), ACT.Copy)
         gather(1, 0)
         gather(1, 1)

@@ -16,7 +16,8 @@ ACT = mybir.ActivationFunctionType
 ALU = mybir.AluOpType
 
 LOADS = (((0, 1024), (1024, 1024)), ((0, 1024), (1024, 512), (1536, 512)))
-PIECES = ((0, 512), (512, 256), (768, 256))
+PIECES = ((0, 256), (256, 256), (512, 256), (768, 256))
+PLAIN = (0, 1)
 
 
 def tile_picked_sub_lin_relu2_sub_e_kernel(tc, xT, w, b, gate, offs, pos1, pos2, pos3, out):
@@ -36,6 +37,7 @@ def tile_picked_sub_lin_relu2_sub_e_kernel(tc, xT, w, b, gate, offs, pos1, pos2,
         w_scales = keep.tile([P, N], U8, name="w_scales", align_bytes=64)
         bias = keep.tile([P, 1], F32, name="bias")
         grouped = [keep.tile([P, n, 4], BF16, name=f"grouped_{i}", align_bytes=64) for i, (a, n) in enumerate(PIECES)]
+        planar = {i: keep.tile([P, 2, PIECES[i][1]], U32, name=f"planar_{i}") for i in PLAIN}
         codes = [keep.tile([P, n], U32, name=f"codes_{i}", align_bytes=64) for i, (a, n) in enumerate(PIECES)]
         scales = [keep.tile([P, n], U8, name=f"scales_{i}", align_bytes=64) for i, (a, n) in enumerate(PIECES)]
         rect = [keep.tile([P, n], F32, name=f"rect_{i}") for i, (a, n) in enumerate(PIECES)]
@@ -71,7 +73,14 @@ def tile_picked_sub_lin_relu2_sub_e_kernel(tc, xT, w, b, gate, offs, pos1, pos2,
             a, n = PIECES[i]
             words = grouped[i][:].rearrange("p n k -> p (n k)").bitcast(U32).rearrange("p (n u) -> p n u", u=2)
             window = pairs[u][:].rearrange("p t e -> p (t e)").bitcast(U32)
-            nc.vector.tensor_copy(words[:, :, u], window.indirect(offsets[:, a // 16 : (a + n) // 16]))
+            dst = planar[i][:, u, :] if i in PLAIN else words[:, :, u]
+            nc.vector.tensor_copy(dst, window.indirect(offsets[:, a // 16 : (a + n) // 16]))
+
+        def interleave(i):
+            src = planar[i][:].rearrange("p u n -> p (u n)").bitcast(BF16)
+            nc.scalar.copy(
+                grouped[i][:].rearrange("p n (u e) -> p n u e", u=2), src.rearrange("p (u n e) -> p n u e", u=2, e=2)
+            )
 
         def quantize(i):
             nc.vector.quantize_mx(
@@ -106,32 +115,32 @@ def tile_picked_sub_lin_relu2_sub_e_kernel(tc, xT, w, b, gate, offs, pos1, pos2,
         cast("V", 0, 0, 640, 1024)
         cast("S", 0, 1, 0, 352)
         cast("V", 0, 1, 352, 1024)
-        for i in range(3):
+        for i in range(4):
             gather(0, i)
         cast("S", 1, 0, 0, 512)
         cast("S", 1, 0, 512, 1024)
         cast("V", 1, 1, 0, 512)
         cast("V", 1, 2, 0, 352)
         cast("S", 1, 2, 352, 512)
-        nc.scalar.activation(w_grouped[:], w_raw[:].rearrange("p j n -> p n j"), ACT.Copy)
-        gather(1, 0)
-        gather(1, 1)
+        nc.gpsimd.tensor_scalar(w_grouped[:], w_raw[:].rearrange("p j n -> p n j"), 1.0, 0.0, ALU.mult, ALU.add)
+        for i in range(4):
+            gather(1, i)
+        interleave(0)
+        interleave(1)
         nc.vector.quantize_mx(
             out=w_codes[:].bitcast(FP8X4), scales=w_scales[:], in_=w_grouped[:].rearrange("p n j -> p (n j)")
         )
-        quantize(0)
-        multiply(0)
-        relu("S", 0, 0, 512)
-        square("S", 0, 0, 512)
-        gather(1, 2)
-        quantize(1)
-        multiply(1)
-        quantize(2)
-        multiply(2)
+        for i in (0, 2, 3, 1):
+            quantize(i)
+            multiply(i)
+        relu("S", 0, 0, 256)
+        square("S", 0, 0, 256)
+        relu("S", 2, 0, 256)
+        square("S", 2, 0, 256)
+        relu("V", 3, 0, 256)
         relu("V", 1, 0, 256)
-        relu("V", 2, 0, 256)
-        square("V", 1, 0, 256)
-        square("V", 2, 0, 256)
+        square("V", 3, 0, 256)
+        square("S", 1, 0, 256)
 
         for d in range(D):
             nc.vector.tensor_tensor(turns[d][:], y[:].indirect(lists[d][:]), gates[d][:], ALU.mult)

@@ -1,6 +1,7 @@
 from contextlib import ExitStack
 
 import concourse.mybir as mybir
+from concourse.masks import make_identity
 
 K, T, D, S, V, N = 512, 2048, 3, 1024, 512, 128
 P = 128
@@ -15,9 +16,10 @@ FP8X4 = mybir.dt.float8_e4m3fn_x4
 ACT = mybir.ActivationFunctionType
 ALU = mybir.AluOpType
 
-LOADS = (((0, 1024), (1024, 1024)), ((0, 1024), (1024, 512), (1536, 512)))
+LOADS = (((0, 1024), (1024, 1024)), ((0, 1024), (1024, 640), (1664, 384)))
 PIECES = ((0, 256), (256, 256), (512, 256), (768, 256))
-PLAIN = (0, 1)
+WARM = 24
+PLAIN = {0: "S", 1: "G"}
 
 
 def tile_picked_sub_lin_relu2_sub_e_kernel(tc, xT, w, b, gate, offs, pos1, pos2, pos3, out):
@@ -46,6 +48,10 @@ def tile_picked_sub_lin_relu2_sub_e_kernel(tc, xT, w, b, gate, offs, pos1, pos2,
         partial = keep.tile([P, V], F32, name="partial")
         result = keep.tile([P, V], F32, name="result")
         acc = [psum.tile([P, n], F32, name=f"acc_{i}") for i, (a, n) in enumerate(PIECES)]
+
+        identity = keep.tile([P, P], BF16, name="identity", align_bytes=64)
+        make_identity(nc, identity[:])
+        warm = [psum.tile([P, 8, P], BF16, name=f"warm_{i}") for i in range(2)]
 
         x_view = xT.rearrange("(p u j) t -> u p j t", u=2, j=2)
         for u in range(2):
@@ -78,9 +84,12 @@ def tile_picked_sub_lin_relu2_sub_e_kernel(tc, xT, w, b, gate, offs, pos1, pos2,
 
         def interleave(i):
             src = planar[i][:].rearrange("p u n -> p (u n)").bitcast(BF16)
-            nc.scalar.copy(
-                grouped[i][:].rearrange("p n (u e) -> p n u e", u=2), src.rearrange("p (u n e) -> p n u e", u=2, e=2)
-            )
+            dst = grouped[i][:].rearrange("p n (u e) -> p n u e", u=2)
+            src = src.rearrange("p (u n e) -> p n u e", u=2, e=2)
+            if PLAIN[i] == "S":
+                nc.scalar.copy(dst, src)
+            else:
+                nc.gpsimd.tensor_scalar(dst, src, 1.0, 0.0, ALU.mult, ALU.add)
 
         def quantize(i):
             nc.vector.quantize_mx(
@@ -119,10 +128,14 @@ def tile_picked_sub_lin_relu2_sub_e_kernel(tc, xT, w, b, gate, offs, pos1, pos2,
             gather(0, i)
         cast("S", 1, 0, 0, 512)
         cast("S", 1, 0, 512, 1024)
-        cast("V", 1, 1, 0, 512)
-        cast("V", 1, 2, 0, 352)
-        cast("S", 1, 2, 352, 512)
+        cast("V", 1, 1, 0, 640)
+        cast("V", 1, 2, 0, 256)
+        cast("S", 1, 2, 256, 384)
         nc.gpsimd.tensor_scalar(w_grouped[:], w_raw[:].rearrange("p j n -> p n j"), 1.0, 0.0, ALU.mult, ALU.add)
+        last = pairs[1][:].rearrange("p t e -> p (t e)")
+        for i in range(WARM):
+            at = 2 * 1664 + (i % 6) * P
+            nc.tensor.transpose(warm[(i // 8) % 2][:, i % 8, :], last[:, at : at + P], identity[:])
         for i in range(4):
             gather(1, i)
         interleave(0)
@@ -130,17 +143,18 @@ def tile_picked_sub_lin_relu2_sub_e_kernel(tc, xT, w, b, gate, offs, pos1, pos2,
         nc.vector.quantize_mx(
             out=w_codes[:].bitcast(FP8X4), scales=w_scales[:], in_=w_grouped[:].rearrange("p n j -> p (n j)")
         )
-        for i in (0, 2, 3, 1):
+        for i in (2, 3, 0, 1):
             quantize(i)
             multiply(i)
-        relu("S", 0, 0, 256)
-        square("S", 0, 0, 256)
         relu("S", 2, 0, 256)
         square("S", 2, 0, 256)
-        relu("V", 3, 0, 256)
+        relu("S", 3, 0, 256)
+        square("S", 3, 0, 256)
+        relu("V", 0, 0, 256)
         relu("V", 1, 0, 256)
-        square("V", 3, 0, 256)
-        square("S", 1, 0, 256)
+        square("S", 0, 0, 256)
+        square("V", 1, 0, 128)
+        square("S", 1, 128, 256)
 
         for d in range(D):
             nc.vector.tensor_tensor(turns[d][:], y[:].indirect(lists[d][:]), gates[d][:], ALU.mult)

@@ -16,7 +16,7 @@ FP8X4 = mybir.dt.float8_e4m3fn_x4
 ACT = mybir.ActivationFunctionType
 ALU = mybir.AluOpType
 
-LOADS = (((0, 1024), (1024, 1024)), ((0, 1024), (1024, 640), (1664, 384)))
+LOADS = (((0, 1024), (1024, 1024)), ((0, 1024), (1024, 768), (1792, 256)))
 PIECES = ((0, 256), (256, 256), (512, 256), (768, 256))
 WARM = 24
 PLAIN = {0: "S", 1: "G"}
@@ -129,12 +129,13 @@ def tile_picked_sub_lin_relu2_sub_e_kernel(tc, xT, w, b, gate, offs, pos1, pos2,
         cast("S", 1, 0, 0, 512)
         cast("S", 1, 0, 512, 1024)
         cast("V", 1, 1, 0, 640)
-        cast("V", 1, 2, 0, 256)
-        cast("S", 1, 2, 256, 384)
+        cast("S", 1, 1, 640, 768)
+        cast("V", 1, 2, 0, 176)
+        cast("S", 1, 2, 176, 256)
         nc.gpsimd.tensor_scalar(w_grouped[:], w_raw[:].rearrange("p j n -> p n j"), 1.0, 0.0, ALU.mult, ALU.add)
         last = pairs[1][:].rearrange("p t e -> p (t e)")
         for i in range(WARM):
-            at = 2 * 1664 + (i % 6) * P
+            at = 2 * 1792 + (i % 4) * P
             nc.tensor.transpose(warm[(i // 8) % 2][:, i % 8, :], last[:, at : at + P], identity[:])
         for i in range(4):
             gather(1, i)

from contextlib import ExitStack

import concourse.mybir as mybir
from concourse.masks import make_identity

K, T, D, S, V, N = 512, 2048, 3, 1024, 512, 128
P = 128
FLOPS = 2 * K * N * S

F32 = mybir.dt.float32
BF16 = mybir.dt.bfloat16
U32 = mybir.dt.uint32
U16 = mybir.dt.uint16
U8 = mybir.dt.uint8
FP8X4 = mybir.dt.float8_e4m3fn_x4
ACT = mybir.ActivationFunctionType
ALU = mybir.AluOpType

LOADS = (((0, 1024), (1024, 1024)), ((0, 1024), (1024, 768), (1792, 256)))
PIECES = ((0, 256), (256, 256), (512, 256), (768, 256))
WARM = 24
PLAIN = {0: "S", 1: "G"}


def tile_picked_sub_lin_relu2_sub_e_kernel(tc, xT, w, b, gate, offs, pos1, pos2, pos3, out):
    nc = tc.nc
    with ExitStack() as ctx:
        keep = ctx.enter_context(tc.tile_pool(name="keep", bufs=1))
        psum = ctx.enter_context(tc.psum_pool(name="psum", bufs=1))

        raw = [[keep.tile([P, 2, n], F32, name=f"raw_{u}_{a}") for (a, n) in LOADS[u]] for u in range(2)]
        pairs = [keep.tile([P, T, 2], BF16, name=f"pairs_{u}", align_bytes=64) for u in range(2)]
        offsets = keep.tile([P, S // 16], U16, name="offsets")
        lists = [keep.tile([P, V // 16], U16, name=f"list_{d}") for d in range(D)]
        gates = [keep.tile([P, V], F32, name=f"gate_{d}") for d in range(D)]
        w_raw = keep.tile([P, 4, N], F32, name="w_raw")
        w_grouped = keep.tile([P, N, 4], BF16, name="w_grouped", align_bytes=64)
        w_codes = keep.tile([P, N], U32, name="w_codes", align_bytes=64)
        w_scales = keep.tile([P, N], U8, name="w_scales", align_bytes=64)
        bias = keep.tile([P, 1], F32, name="bias")
        grouped = [keep.tile([P, n, 4], BF16, name=f"grouped_{i}", align_bytes=64) for i, (a, n) in enumerate(PIECES)]
        planar = {i: keep.tile([P, 2, PIECES[i][1]], U32, name=f"planar_{i}") for i in PLAIN}
        codes = [keep.tile([P, n], U32, name=f"codes_{i}", align_bytes=64) for i, (a, n) in enumerate(PIECES)]
        scales = [keep.tile([P, n], U8, name=f"scales_{i}", align_bytes=64) for i, (a, n) in enumerate(PIECES)]
        rect = [keep.tile([P, n], F32, name=f"rect_{i}") for i, (a, n) in enumerate(PIECES)]
        y = keep.tile([P, S], F32, name="y")
        turns = [keep.tile([P, V], F32, name=f"turn_{d}") for d in range(D)]
        partial = keep.tile([P, V], F32, name="partial")
        result = keep.tile([P, V], F32, name="result")
        acc = [psum.tile([P, n], F32, name=f"acc_{i}") for i, (a, n) in enumerate(PIECES)]

        identity = keep.tile([P, P], BF16, name="identity", align_bytes=64)
        make_identity(nc, identity[:])
        warm = [psum.tile([P, 8, P], BF16, name=f"warm_{i}") for i in range(2)]

        x_view = xT.rearrange("(p u j) t -> u p j t", u=2, j=2)
        for u in range(2):
            for c, (a, n) in enumerate(LOADS[u]):
                nc.sync.dma_start(raw[u][c][:], x_view[u, :, :, a : a + n])
            if u == 0:
                nc.sync.dma_start(offsets[:], offs)
        nc.sync.dma_start(w_raw[:], w.rearrange("(p j) n -> p j n", j=4))
        nc.sync.dma_start(bias[:], b)
        for d, pos in enumerate((pos1, pos2, pos3)):
            nc.sync.dma_start(lists[d][:], pos)
        for d in range(D):
            nc.sync.dma_start(gates[d][:], gate[d])

        def cast(engine, u, c, lo, hi):
            a, n = LOADS[u][c]
            dst = pairs[u][:, a + lo : a + hi, :]
            src = raw[u][c][:, :, lo:hi].rearrange("p j t -> p t j")
            if engine == "S":
                nc.scalar.activation(dst, src, ACT.Copy)
            else:
                nc.vector.tensor_copy(dst, src)

        def gather(u, i):
            a, n = PIECES[i]
            words = grouped[i][:].rearrange("p n k -> p (n k)").bitcast(U32).rearrange("p (n u) -> p n u", u=2)
            window = pairs[u][:].rearrange("p t e -> p (t e)").bitcast(U32)
            dst = planar[i][:, u, :] if i in PLAIN else words[:, :, u]
            nc.vector.tensor_copy(dst, window.indirect(offsets[:, a // 16 : (a + n) // 16]))

        def interleave(i):
            src = planar[i][:].rearrange("p u n -> p (u n)").bitcast(BF16)
            dst = grouped[i][:].rearrange("p n (u e) -> p n u e", u=2)
            src = src.rearrange("p (u n e) -> p n u e", u=2, e=2)
            if PLAIN[i] == "S":
                nc.scalar.copy(dst, src)
            else:
                nc.gpsimd.tensor_scalar(dst, src, 1.0, 0.0, ALU.mult, ALU.add)

        def quantize(i):
            nc.vector.quantize_mx(
                out=codes[i][:].bitcast(FP8X4), scales=scales[i][:], in_=grouped[i][:].rearrange("p n k -> p (n k)")
            )

        def multiply(i):
            nc.tensor.matmul_mx(
                out=acc[i][:],
                lhsT=w_codes[:].bitcast(FP8X4),
                lhsT_scale=w_scales[:],
                rhs=codes[i][:].bitcast(FP8X4),
                rhs_scale=scales[i][:],
                start=True,
                stop=True,
            )

        def relu(engine, i, lo, hi):
            if engine == "S":
                nc.scalar.activation(rect[i][:, lo:hi], acc[i][:, lo:hi], ACT.Relu, bias=bias[:, 0:1])
            else:
                nc.vector.tensor_scalar(rect[i][:, lo:hi], acc[i][:, lo:hi], bias[:, 0:1], 0.0, ALU.add, ALU.max)

        def square(engine, i, lo, hi):
            a, n = PIECES[i]
            if engine == "S":
                nc.scalar.activation(y[:, a + lo : a + hi], rect[i][:, lo:hi], ACT.Square)
            else:
                nc.vector.tensor_tensor(y[:, a + lo : a + hi], rect[i][:, lo:hi], rect[i][:, lo:hi], ALU.mult)

        cast("S", 0, 0, 0, 640)
        cast("V", 0, 0, 640, 1024)
        cast("S", 0, 1, 0, 352)
        cast("V", 0, 1, 352, 1024)
        for i in range(4):
            gather(0, i)
        cast("S", 1, 0, 0, 512)
        cast("S", 1, 0, 512, 1024)
        cast("V", 1, 1, 0, 640)
        cast("S", 1, 1, 640, 768)
        cast("V", 1, 2, 0, 176)
        cast("S", 1, 2, 176, 256)
        nc.gpsimd.tensor_scalar(w_grouped[:], w_raw[:].rearrange("p j n -> p n j"), 1.0, 0.0, ALU.mult, ALU.add)
        last = pairs[1][:].rearrange("p t e -> p (t e)")
        for i in range(WARM):
            at = 2 * 1792 + (i % 4) * P
            nc.tensor.transpose(warm[(i // 8) % 2][:, i % 8, :], last[:, at : at + P], identity[:])
        for i in range(4):
            gather(1, i)
        interleave(0)
        interleave(1)
        nc.vector.quantize_mx(
            out=w_codes[:].bitcast(FP8X4), scales=w_scales[:], in_=w_grouped[:].rearrange("p n j -> p (n j)")
        )
        for i in (2, 3, 0, 1):
            quantize(i)
            multiply(i)
        relu("S", 2, 0, 256)
        square("S", 2, 0, 256)
        relu("S", 3, 0, 256)
        square("S", 3, 0, 256)
        relu("V", 0, 0, 256)
        relu("V", 1, 0, 256)
        square("S", 0, 0, 256)
        square("V", 1, 0, 128)
        square("S", 1, 128, 256)

        for d in range(D):
            nc.vector.tensor_tensor(turns[d][:], y[:].indirect(lists[d][:]), gates[d][:], ALU.mult)
        halves = (slice(0, 256), slice(256, 512))
        for h in halves:
            nc.vector.tensor_tensor(partial[:, h], turns[0][:, h], turns[1][:, h], ALU.add)
        for h in halves:
            nc.vector.tensor_tensor(result[:, h], partial[:, h], turns[2][:, h], ALU.add)
            nc.sync.dma_start(out[:, h], result[:, h])
